import numpy as np
import ml_dtypes


def mxq(x, axis, fmt="e4m3"):
    dtype, down = {"e4m3": (ml_dtypes.float8_e4m3fn, 7), "e5m2": (ml_dtypes.float8_e5m2, 14)}[fmt]
    v = np.moveaxis(np.asarray(x, np.float32).astype(ml_dtypes.bfloat16).astype(np.float64), axis, -1)
    blocks = v.reshape(v.shape[:-1] + (-1, 32))
    amax = np.abs(blocks).max(-1, keepdims=True)
    byte = np.maximum(np.where(amax > 0, np.frexp(amax)[1] - 1 + 127, 0) - down, 1)
    scale = np.exp2(byte - 127.0)
    codes = (blocks / scale).astype(np.float32).astype(dtype).astype(np.float64)
    return np.moveaxis((codes * scale).reshape(v.shape), -1, axis)


WIDE = False


def mx_kscale(k):
    if not WIDE:
        return np.ones(k)
    levels = np.array([10, -10, 5, -5, 0])
    if k % 512:
        return np.exp2(np.random.permutation(np.resize(levels, k // 32))).repeat(32)
    a = np.empty((k // 512, 16))
    for p in range(k // 512):
        a[p, :8] = np.random.permutation(np.resize(levels, 8))
        for g in range(8):
            far = levels[np.abs(levels - a[p, g]) >= 10]
            a[p, g + 8] = far[np.random.randint(len(far))]
    return np.exp2(a.ravel()).repeat(32)


def f64(x):
    return np.asarray(x).astype(np.float64)


def striped(idx):
    return np.tile(idx.reshape(-1, 16).T, (8, 1)).astype(np.uint16)


def unstriped(offs):
    return offs[:16].T.reshape(-1).astype(np.int64)


def striped8(idx):
    return np.concatenate([x.reshape(-1, 16).T for x in idx]).astype(np.uint16)


def runs(offs, k):
    lists = np.stack([offs[16 * r : 16 * r + 16].T.reshape(-1) for r in range(8)]).astype(np.int64)
    return lists[np.arange(k) % 512 // 64]


def pack_weight(w):
    k, n = w.shape
    w = f64(np.asarray(w, np.float32).astype(ml_dtypes.bfloat16)).reshape(k // 32, 32, n)
    amax = np.abs(w).max(1)
    byte = np.clip(np.where(amax > 0, np.frexp(amax)[1] - 1 + 127 - 7, 1), 1, 254)
    scaled = (w * np.exp2(127.0 - byte)[:, None, :]).reshape(k, n).astype(np.float32)
    words = np.ascontiguousarray(scaled.reshape(k // 512, 128, 4, n).transpose(0, 1, 3, 2)).astype(ml_dtypes.float8_e4m3fn).view(np.uint8)
    return words, np.ascontiguousarray(byte.astype(np.uint8).reshape(k // 512, 16, n))


def unpack_weight(words, scales):
    g, p, n, _ = words.shape
    vals = np.ascontiguousarray(words).view(ml_dtypes.float8_e4m3fn).astype(np.float64) * np.repeat(np.exp2(scales.astype(np.float64) - 127.0), 8, axis=1)[..., None]
    return vals.transpose(0, 1, 3, 2).reshape(g * 512, n)


E2M1 = np.array([0.0, 0.5, 1.0, 1.5, 2.0, 3.0, 4.0, 6.0, -0.0, -0.5, -1.0, -1.5, -2.0, -3.0, -4.0, -6.0])


def pack_fp4(w):
    k, n = w.shape
    w = f64(np.asarray(w, np.float32).astype(ml_dtypes.bfloat16)).reshape(k // 32, 32, n)
    amax = np.abs(w).max(1)
    mant, ex = np.frexp(amax / 6.0)
    byte = np.clip(np.where(amax > 0, np.where(mant > 0.5, ex, ex - 1) + 127, 1), 1, 254)
    scaled = (w * np.exp2(127.0 - byte)[:, None, :]).reshape(k, n).astype(np.float32)
    c = np.ascontiguousarray(scaled.reshape(k // 512, 128, 4, n).transpose(0, 1, 3, 2)).astype(ml_dtypes.float4_e2m1fn).view(np.uint8) & 0xF
    words = (c[..., 0::2] | (c[..., 1::2] << 4)).reshape(k // 512, 128, 2 * n)
    return np.ascontiguousarray(words), np.ascontiguousarray(byte.astype(np.uint8).reshape(k // 512, 16, n))


def unpack_fp4(words, scales):
    g, _, n = scales.shape
    words = np.ascontiguousarray(words).reshape(g, 128, n, 2)
    nib = np.empty((g, 128, n, 4), np.uint8)
    nib[..., 0::2] = words & 0xF
    nib[..., 1::2] = words >> 4
    vals = E2M1[nib] * np.repeat(np.exp2(scales.astype(np.float64) - 127.0), 8, axis=1)[..., None]
    return vals.transpose(0, 1, 3, 2).reshape(g * 512, n)


K, T, S, N, G, H, W, U = 512, 1024, 256, 512, 2048, 512, 128, 1024


def setup_inputs():
    n = np.random.standard_normal
    s = mx_kscale(K)[:, None]
    u = mx_kscale(K)
    packed_xT = pack_weight(n((K, T)) * s)
    packed_dT = pack_weight(n((K, G)) / s)
    packed_w1 = pack_fp4(n((H, N)) / np.sqrt(H) / u[:, None])
    perm = np.random.permutation(S)
    return {
        "x_words": packed_xT[0],
        "x_scales": packed_xT[1],
        "d_words": packed_dT[0],
        "d_scales": packed_dT[1],
        "gn": (np.random.uniform(0.5, 1.5, (H, 1)) * u[:, None]).astype(np.float32),
        "w1_words": packed_w1[0],
        "w1_scales": packed_w1[1],
        "offs": striped(np.random.permutation(T)[:S]),
        "ka": striped8(np.random.randint(0, G, (8, H))),
        "kb": striped8(np.random.randint(0, G, (8, H))),
        "n1": striped(perm[:W]),
        "n2": striped(perm[W:]),
        "n3": striped(np.random.permutation(S)),
        "n4": striped(np.random.permutation(U)[:S]),
        "n5": striped(np.random.permutation(S)),
    }


def reference(x_words, x_scales, d_words, d_scales, gn, w1_words, w1_scales, offs, ka, kb, n1, n2, n3, n4, n5):
    d_ka = unpack_weight(d_words, d_scales)[np.arange(K)[:, None], runs(ka, K)]
    xq = unpack_weight(x_words, x_scales)[:, unstriped(offs)]
    d_kb = unpack_weight(d_words, d_scales)[np.arange(K)[:, None], runs(kb, K)]
    h = 0.0625 * (d_ka.T @ xq + d_kb.T @ xq)
    pa = h[:, unstriped(n1)]
    pb = h[:, unstriped(n2)]
    rb = np.minimum(pa, pb)
    ra = np.maximum(pa, pb)
    ds = np.zeros((H, S))
    ds[:, unstriped(n1)] = ra
    dt = ds.copy()
    dt[:, unstriped(n2)] = rb
    z = f64(gn) * (dt - dt[:, unstriped(n3)])
    h2 = unpack_fp4(w1_words, w1_scales).T @ mxq(z, 0, "e4m3")
    nw = np.maximum(h2, h2[:, unstriped(n5)])
    out = np.zeros((N, U))
    out[:, unstriped(n4)] = nw
    return out

@@ -1,0 +1,190 @@
+from contextlib import ExitStack
+
+import concourse.mybir as mybir
+
+K, T, S, N, G, H, W, U = 512, 1024, 256, 512, 2048, 512, 128, 1024
+FLOPS = 2 * 2 * K * H * S + 2 * H * N * S
+
+F32 = mybir.dt.float32
+BF16 = mybir.dt.bfloat16
+I32 = mybir.dt.int32
+U32 = mybir.dt.uint32
+U16 = mybir.dt.uint16
+U8 = mybir.dt.uint8
+FP8X4 = mybir.dt.float8_e4m3fn_x4
+FP4X4 = mybir.dt.float4_e2m1fn_x4
+ALU = mybir.AluOpType
+COPY = mybir.ActivationFunctionType.Copy
+P = 128
+
+
+def tile_picked_aqlorddpags_none_p_kernel(
+    tc, x_words, x_scales, d_words, d_scales, gn, w1_words, w1_scales, offs, ka, kb, n1, n2, n3, n4, n5, out
+):
+    nc = tc.nc
+    with ExitStack() as ctx:
+        keep = ctx.enter_context(tc.tile_pool(name="keep", bufs=1))
+        psum = ctx.enter_context(tc.psum_pool(name="psum", bufs=1))
+
+        def load_list(src, name):
+            tl = keep.tile([P, src.shape[1]], U16, name=name)
+            nc.sync.dma_start(tl[:], src)
+            return tl
+
+        d_sc = keep.tile([P, G], U8, name="d_sc", align_bytes=64)
+        x_sc = keep.tile([P, T], U8, name="x_sc", align_bytes=64)
+        w_sc = keep.tile([P, N], U8, name="w_sc", align_bytes=64)
+        nc.vector.memset(d_sc[:].bitcast(I32), 0)
+        nc.vector.memset(x_sc[:].bitcast(I32), 0)
+        for e in range(2):
+            nc.scalar.dma_start(d_sc[e:P:16, :].bitcast(I32), d_scales[0][e:16:2, :].bitcast(I32))
+        ka_t = load_list(ka, "ka_t")
+        kb_t = load_list(kb, "kb_t")
+        d_w = keep.tile([P, G], I32, name="d_w", align_bytes=64)
+        x_w = keep.tile([P, T], I32, name="x_w", align_bytes=64)
+        nc.sync.dma_start(d_w[:], d_words[0].rearrange("p n t -> p (n t)").bitcast(I32))
+        offs_t = load_list(offs, "offs_t")
+        nc.sync.dma_start(x_w[:], x_words[0].rearrange("p n t -> p (n t)").bitcast(I32))
+        for j in range(4):
+            nc.sync.dma_start(x_sc[j:P:32, :].bitcast(I32), x_scales[0][j:16:4, :].bitcast(I32))
+        n1_t = load_list(n1, "n1_t")
+        n2_t = load_list(n2, "n2_t")
+        n3_t = load_list(n3, "n3_t")
+        n5_t = load_list(n5, "n5_t")
+        n4_t = load_list(n4, "n4_t")
+
+        pages = [keep.tile([P, U], F32, name="page%d" % i) for i in range(4)]
+        nc.vector.memset(w_sc[:].bitcast(I32), 0)
+        nc.gpsimd.memset(pages[0][:], 0.0)
+        nc.gpsimd.memset(pages[1][:], 0.0)
+        nc.vector.memset(pages[2][:], 0.0)
+        nc.vector.memset(pages[3][:], 0.0)
+
+        gn_t = keep.tile([P, 4], F32, name="gn_t")
+        w_w = keep.tile([P, 2 * N], U8, name="w_w", align_bytes=64)
+        nc.gpsimd.dma_start(gn_t[:], gn.rearrange("(p t) o -> p (t o)", t=4))
+        nc.gpsimd.dma_start(w_w[:].bitcast(I32), w1_words[0].bitcast(I32))
+        for j in range(4):
+            nc.gpsimd.dma_start(w_sc[j:P:32, :].bitcast(I32), w1_scales[0][j:16:4, :].bitcast(I32))
+
+        db_raw = keep.tile([P, 2 * H], U8, name="db_raw", align_bytes=64)
+        db = keep.tile([P, 2 * H], U8, name="db", align_bytes=64)
+        nc.vector.tensor_copy(db_raw[:, 0:H], d_sc[:].indirect(ka_t[:]))
+        nc.vector.tensor_copy(db_raw[:, H : 2 * H], d_sc[:].indirect(kb_t[:]))
+        nc.vector.tensor_copy(
+            db[:].rearrange("p (l t m) -> p l m t", l=2, t=4), db_raw[:].rearrange("p (l m t) -> p l m t", l=2, t=4)
+        )
+        for e in range(2):
+            nc.scalar.dma_start(db[2 + e : P : 32, :].bitcast(I32), db[16 + e : P : 32, :].bitcast(I32))
+
+        dw = []
+        for l, lst in enumerate((ka_t, kb_t)):
+            raw = keep.tile([P, H], U32, name="dw_raw%d" % l, align_bytes=64)
+            dealt = keep.tile([P, H], U32, name="dw%d" % l, align_bytes=64)
+            nc.vector.tensor_copy(raw[:], d_w[:].bitcast(U32).indirect(lst[:]))
+            dw.append((raw, dealt))
+        for raw, dealt in dw:
+            nc.vector.tensor_copy(
+                dealt[:].rearrange("p (t m) -> p m t", t=4), raw[:].rearrange("p (m t) -> p m t", t=4)
+            )
+        xw = keep.tile([P, S], U32, name="xw", align_bytes=64)
+        xb = keep.tile([P, S], U8, name="xb", align_bytes=64)
+        nc.vector.tensor_copy(xw[:], x_w[:].bitcast(U32).indirect(offs_t[:]))
+        nc.vector.tensor_copy(xb[:], x_sc[:].indirect(offs_t[:]))
+
+        hs = []
+        for t in range(4):
+            acc = psum.tile([P, S], F32, name="h_acc%d" % t)
+            for l in range(2):
+                nc.tensor.matmul_mx(
+                    out=acc[:],
+                    lhsT=dw[l][1][:, t * P : (t + 1) * P].bitcast(FP8X4),
+                    lhsT_scale=db[:, l * H + t * P : l * H + (t + 1) * P],
+                    rhs=xw[:].bitcast(FP8X4),
+                    rhs_scale=xb[:],
+                    start=(l == 0),
+                    stop=(l == 1),
+                )
+            h = keep.tile([P, S], F32, name="h%d" % t)
+            nc.vector.tensor_scalar(h[:], acc[:], 0.0625, None, ALU.mult)
+            hs.append(h)
+
+        zq = keep.tile([P, S, 4], BF16, name="zq", align_bytes=64)
+        pa = [keep.tile([P, W], F32, name="pa%d" % t) for t in range(4)]
+        pb = [keep.tile([P, W], F32, name="pb%d" % t) for t in range(4)]
+        ra = [keep.tile([P, W], F32, name="ra%d" % t) for t in range(4)]
+        rb = [keep.tile([P, W], F32, name="rb%d" % t) for t in range(4)]
+        dt = [keep.tile([P, S], F32, name="dt%d" % t) for t in range(4)]
+        far = [keep.tile([P, S], F32, name="far%d" % t) for t in range(4)]
+        dif = [keep.tile([P, S], F32, name="dif%d" % t) for t in range(4)]
+
+        def pick(t):
+            nc.scalar.activation(pa[t][:], hs[t][:].indirect(n1_t[:]), COPY)
+            nc.scalar.activation(pb[t][:], hs[t][:].indirect(n2_t[:]), COPY)
+            nc.vector.tensor_tensor(ra[t][:], pa[t][:], pb[t][:], ALU.max)
+            nc.vector.tensor_tensor(rb[t][:], pa[t][:], pb[t][:], ALU.min)
+
+        def put(t):
+            nc.scalar.activation(dt[t][:].indirect(n1_t[:]), ra[t][:], COPY)
+            nc.scalar.activation(dt[t][:].indirect(n2_t[:]), rb[t][:], COPY)
+
+        def differ(t, c):
+            cols = slice(c * W, (c + 1) * W)
+            nc.scalar.activation(far[t][:, cols], dt[t][:].indirect(n3_t[:, c * 8 : (c + 1) * 8]), COPY)
+            nc.vector.tensor_tensor(dif[t][:, cols], dt[t][:, cols], far[t][:, cols], ALU.subtract)
+            nc.vector.tensor_scalar(zq[:, cols, t], dif[t][:, cols], gn_t[:, t : t + 1], None, ALU.mult)
+
+        pick(0)
+        for t in range(4):
+            if t + 1 < 4:
+                pick(t + 1)
+            put(t)
+            if t > 0:
+                differ(t - 1, 0)
+        differ(3, 0)
+
+        zc = keep.tile([P, S], U32, name="zc", align_bytes=64)
+        zs = keep.tile([P, S], U8, name="zs", align_bytes=64)
+        acc2 = [[psum.tile([P, W], F32, name="o_acc%d_%d" % (c, m), tag="o_acc%d" % m) for m in range(4)] for c in range(1)]
+        h2 = [keep.tile([P, S], F32, name="h2_%d" % m) for m in range(4)]
+
+        def second(c):
+            cols = slice(c * W, (c + 1) * W)
+            nc.vector.quantize_mx(
+                out=zc[:, cols].bitcast(FP8X4), scales=zs[:, cols], in_=zq[:, cols, :].rearrange("p c t -> p (c t)")
+            )
+            for m in range(4):
+                acc = acc2[0][m] if c == 0 else psum.tile([P, W], F32, name="o_accb%d" % m, tag="h_acc%d" % m)
+                nc.tensor.matmul_mx(
+                    out=acc[:],
+                    lhsT=w_w[:, 2 * P * m : 2 * P * (m + 1)].bitcast(FP4X4),
+                    lhsT_scale=w_sc[:, P * m : P * (m + 1)],
+                    rhs=zc[:, cols].bitcast(FP8X4),
+                    rhs_scale=zs[:, cols],
+                    start=True,
+                    stop=True,
+                )
+                nc.vector.tensor_copy(h2[m][:, cols], acc[:])
+
+        second(0)
+        for t in range(4):
+            differ(t, 1)
+        second(1)
+
+        near = [keep.tile([P, S], F32, name="near%d" % m) for m in range(4)]
+        nw = [keep.tile([P, S], F32, name="nw%d" % m) for m in range(4)]
+
+        def look(m):
+            for c in range(2):
+                nc.scalar.activation(near[m][:, c * W : (c + 1) * W], h2[m][:].indirect(n5_t[:, c * 8 : (c + 1) * 8]), COPY)
+            nc.vector.tensor_tensor(nw[m][:], h2[m][:], near[m][:], ALU.max)
+
+        def leave(m):
+            nc.scalar.activation(pages[m][:].indirect(n4_t[:]), nw[m][:], COPY)
+            nc.sync.dma_start(out[m * P : (m + 1) * P, :], pages[m][:])
+
+        look(0)
+        for m in range(4):
+            if m + 1 < 4:
+                look(m + 1)
+            leave(m)

@@ -16,6 +16,9 @@ FP4X4 = mybir.dt.float4_e2m1fn_x4
 ALU = mybir.AluOpType
 COPY = mybir.ActivationFunctionType.Copy
 P = 128
+HP = 64
+HALF = H // 2
+SPARE = 16
 
 
 def tile_picked_aqlorddpags_none_p_kernel(
@@ -24,6 +27,7 @@ def tile_picked_aqlorddpags_none_p_kernel(
     nc = tc.nc
     with ExitStack() as ctx:
         keep = ctx.enter_context(tc.tile_pool(name="keep", bufs=1))
+        reuse = ctx.enter_context(tc.tile_pool(name="reuse", bufs=1))
         psum = ctx.enter_context(tc.psum_pool(name="psum", bufs=1))
 
         def load_list(src, name):
@@ -31,153 +35,229 @@ def tile_picked_aqlorddpags_none_p_kernel(
             nc.sync.dma_start(tl[:], src)
             return tl
 
-        d_sc = keep.tile([P, G], U8, name="d_sc", align_bytes=64)
-        x_sc = keep.tile([P, T], U8, name="x_sc", align_bytes=64)
-        w_sc = keep.tile([P, N], U8, name="w_sc", align_bytes=64)
-        nc.vector.memset(d_sc[:].bitcast(I32), 0)
-        nc.vector.memset(x_sc[:].bitcast(I32), 0)
-        for e in range(2):
-            nc.scalar.dma_start(d_sc[e:P:16, :].bitcast(I32), d_scales[0][e:16:2, :].bitcast(I32))
-        ka_t = load_list(ka, "ka_t")
-        kb_t = load_list(kb, "kb_t")
-        d_w = keep.tile([P, G], I32, name="d_w", align_bytes=64)
-        x_w = keep.tile([P, T], I32, name="x_w", align_bytes=64)
-        nc.sync.dma_start(d_w[:], d_words[0].rearrange("p n t -> p (n t)").bitcast(I32))
+        def load_scales(src, name):
+            rows = src[0].bitcast(I32)
+            tl = keep.tile([P, src.shape[2]], U8, name=name, align_bytes=64)
+            nc.sync.dma_start(tl[:].bitcast(I32), rows.unsqueeze(1).to_broadcast([16, 8, rows.shape[1]]))
+            return tl
+
+        def load_words(src, tl):
+            nc.sync.dma_start(tl[:], src[0].rearrange("p n t -> p (n t)").bitcast(I32))
+            return tl
+
         offs_t = load_list(offs, "offs_t")
-        nc.sync.dma_start(x_w[:], x_words[0].rearrange("p n t -> p (n t)").bitcast(I32))
-        for j in range(4):
-            nc.sync.dma_start(x_sc[j:P:32, :].bitcast(I32), x_scales[0][j:16:4, :].bitcast(I32))
+        x_sc = load_scales(x_scales, "x_sc")
+        codes = [load_list(ka, "ka_t"), load_list(kb, "kb_t")]
+        d_sc = load_scales(d_scales, "d_sc")
         n1_t = load_list(n1, "n1_t")
         n2_t = load_list(n2, "n2_t")
+        d_w = load_words(d_words, keep.tile([P, G], I32, name="d_w", align_bytes=64))
+        x_w = load_words(x_words, reuse.tile([P, T], I32, name="x_w", offset=0, align_bytes=64))
         n3_t = load_list(n3, "n3_t")
         n5_t = load_list(n5, "n5_t")
         n4_t = load_list(n4, "n4_t")
 
         pages = [keep.tile([P, U], F32, name="page%d" % i) for i in range(4)]
-        nc.vector.memset(w_sc[:].bitcast(I32), 0)
-        nc.gpsimd.memset(pages[0][:], 0.0)
-        nc.gpsimd.memset(pages[1][:], 0.0)
-        nc.vector.memset(pages[2][:], 0.0)
-        nc.vector.memset(pages[3][:], 0.0)
+        nc.gpsimd.memset(pages[0][:].bitcast(I32), 0)
+        nc.gpsimd.memset(pages[1][:].bitcast(I32), 0)
+        nc.vector.memset(pages[2][:].bitcast(I32), 0)
+        nc.vector.memset(pages[3][:].bitcast(I32), 0)
 
-        gn_t = keep.tile([P, 4], F32, name="gn_t")
-        w_w = keep.tile([P, 2 * N], U8, name="w_w", align_bytes=64)
-        nc.gpsimd.dma_start(gn_t[:], gn.rearrange("(p t) o -> p (t o)", t=4))
-        nc.gpsimd.dma_start(w_w[:].bitcast(I32), w1_words[0].bitcast(I32))
-        for j in range(4):
-            nc.gpsimd.dma_start(w_sc[j:P:32, :].bitcast(I32), w1_scales[0][j:16:4, :].bitcast(I32))
+        def pick(dst, window, l, hf):
+            nc.vector.tensor_copy(dst, window.indirect(codes[l][:, hf * 16 : (hf + 1) * 16]))
 
-        db_raw = keep.tile([P, 2 * H], U8, name="db_raw", align_bytes=64)
-        db = keep.tile([P, 2 * H], U8, name="db", align_bytes=64)
-        nc.vector.tensor_copy(db_raw[:, 0:H], d_sc[:].indirect(ka_t[:]))
-        nc.vector.tensor_copy(db_raw[:, H : 2 * H], d_sc[:].indirect(kb_t[:]))
-        nc.vector.tensor_copy(
-            db[:].rearrange("p (l t m) -> p l m t", l=2, t=4), db_raw[:].rearrange("p (l m t) -> p l m t", l=2, t=4)
-        )
-        for e in range(2):
-            nc.scalar.dma_start(db[2 + e : P : 32, :].bitcast(I32), db[16 + e : P : 32, :].bitcast(I32))
+        def pick_half(raw, window, hf):
+            for l in range(2):
+                pick(raw[:, l * HALF : (l + 1) * HALF], window, l, hf)
 
-        dw = []
-        for l, lst in enumerate((ka_t, kb_t)):
-            raw = keep.tile([P, H], U32, name="dw_raw%d" % l, align_bytes=64)
-            dealt = keep.tile([P, H], U32, name="dw%d" % l, align_bytes=64)
-            nc.vector.tensor_copy(raw[:], d_w[:].bitcast(U32).indirect(lst[:]))
-            dw.append((raw, dealt))
-        for raw, dealt in dw:
-            nc.vector.tensor_copy(
-                dealt[:].rearrange("p (t m) -> p m t", t=4), raw[:].rearrange("p (m t) -> p m t", t=4)
-            )
+        def entries(raw, t0):
+            return raw[:, 0:H].rearrange("p (l m t) -> p l m t", l=2, t=4)[:, :, :, t0 : t0 + 2]
+
+        def deal_early(dst, raw):
+            nc.vector.tensor_copy(dst.rearrange("p (l t m) -> p l m t", l=2, t=2), entries(raw, 0))
+
+        def deal_late(dst, raw, hf):
+            view = dst.rearrange("p (l t m) -> p l m t", l=2, t=2)[:, :, hf * HP : (hf + 1) * HP, :]
+            nc.vector.tensor_copy(view, entries(raw, 2))
+
+        def settle(queues, plane):
+            for j, queue in zip(range(1, 4), queues):
+                queue.dma_start(plane[j:P:32, :].bitcast(I32), plane[8 * j : P : 32, :].bitcast(I32))
+
+        sc1 = keep.tile([P, 2 * P + S], U8, name="sc1", align_bytes=64)
+        sc2 = reuse.tile([P, 6 * P], U8, name="sc2", offset=1024, align_bytes=64)
+        w_early = [keep.tile([P, 2 * P], U32, name="w_early%d" % hf, align_bytes=64) for hf in range(2)]
         xw = keep.tile([P, S], U32, name="xw", align_bytes=64)
-        xb = keep.tile([P, S], U8, name="xb", align_bytes=64)
-        nc.vector.tensor_copy(xw[:], x_w[:].bitcast(U32).indirect(offs_t[:]))
-        nc.vector.tensor_copy(xb[:], x_sc[:].indirect(offs_t[:]))
 
-        hs = []
-        for t in range(4):
-            acc = psum.tile([P, S], F32, name="h_acc%d" % t)
+        raw_b0 = keep.tile([P, H + S], U8, name="raw_b0", tag="first", align_bytes=64)
+        nc.vector.tensor_copy(raw_b0[:, H : H + S], x_sc[:].indirect(offs_t[:]))
+        pick_half(raw_b0, d_sc[:], 0)
+        nc.vector.tensor_copy(sc1[:, 2 * P :].bitcast(I32), raw_b0[:, H : H + S].bitcast(I32))
+        deal_early(sc1[:, 0 : 2 * P], raw_b0)
+        settle((nc.sync, nc.scalar, nc.sync), sc1)
+
+        raw_w0 = keep.tile([P, H], U32, name="raw_w0", tag="raw", align_bytes=64)
+        pick_half(raw_w0, d_w[:].bitcast(U32), 0)
+        deal_early(w_early[0][:], raw_w0)
+        nc.vector.tensor_copy(xw[:], x_w[:].bitcast(U32).indirect(offs_t[:]))
+        deal_late(sc2[:, 2 * P :], raw_b0, 0)
+
+        def product(name, words, plane, c0, step):
+            acc = psum.tile([P, S], F32, name=name)
             for l in range(2):
                 nc.tensor.matmul_mx(
                     out=acc[:],
-                    lhsT=dw[l][1][:, t * P : (t + 1) * P].bitcast(FP8X4),
-                    lhsT_scale=db[:, l * H + t * P : l * H + (t + 1) * P],
+                    lhsT=words[:, l * step : l * step + P].bitcast(FP8X4),
+                    lhsT_scale=plane[:, c0 + l * step : c0 + l * step + P],
                     rhs=xw[:].bitcast(FP8X4),
-                    rhs_scale=xb[:],
+                    rhs_scale=sc1[:, 2 * P :],
                     start=(l == 0),
                     stop=(l == 1),
                 )
-            h = keep.tile([P, S], F32, name="h%d" % t)
-            nc.vector.tensor_scalar(h[:], acc[:], 0.0625, None, ALU.mult)
-            hs.append(h)
+            return acc
 
+        hs = [keep.tile([P, S], F32, name="h%d" % t) for t in range(4)]
         zq = keep.tile([P, S, 4], BF16, name="zq", align_bytes=64)
-        pa = [keep.tile([P, W], F32, name="pa%d" % t) for t in range(4)]
-        pb = [keep.tile([P, W], F32, name="pb%d" % t) for t in range(4)]
-        ra = [keep.tile([P, W], F32, name="ra%d" % t) for t in range(4)]
-        rb = [keep.tile([P, W], F32, name="rb%d" % t) for t in range(4)]
-        dt = [keep.tile([P, S], F32, name="dt%d" % t) for t in range(4)]
+        pa = [keep.tile([P, W], F32, name="pa%d" % t, tag="pa%d" % t, align_bytes=64) for t in range(4)]
+        pb = [keep.tile([P, W], F32, name="pb%d" % t, tag="pb%d" % t, align_bytes=64) for t in range(4)]
+        ra = [keep.tile([P, W], F32, name="ra%d" % t) for t in range(2)]
+        ra.extend(reuse.tile([P, W], F32, name="ra%d" % t, offset=4096 + 512 * (t - 2)) for t in (2, 3))
+        rb = {t: keep.tile([P, W], F32, name="rb%d" % t) for t in (0, 2, 3)}
+        rb[1] = reuse.tile([P, W], F32, name="rb_held", offset=4096 + 256)
+        dt = [keep.tile([P, S + SPARE * (t < 2)], F32, name="dt%d" % t) for t in range(4)]
         far = [keep.tile([P, S], F32, name="far%d" % t) for t in range(4)]
-        dif = [keep.tile([P, S], F32, name="dif%d" % t) for t in range(4)]
 
-        def pick(t):
+        def fetch_a(t):
             nc.scalar.activation(pa[t][:], hs[t][:].indirect(n1_t[:]), COPY)
+
+        def fetch_b(t):
             nc.scalar.activation(pb[t][:], hs[t][:].indirect(n2_t[:]), COPY)
             nc.vector.tensor_tensor(ra[t][:], pa[t][:], pb[t][:], ALU.max)
             nc.vector.tensor_tensor(rb[t][:], pa[t][:], pb[t][:], ALU.min)
 
-        def put(t):
+        def put_a(t):
             nc.scalar.activation(dt[t][:].indirect(n1_t[:]), ra[t][:], COPY)
+
+        def put_b(t):
             nc.scalar.activation(dt[t][:].indirect(n2_t[:]), rb[t][:], COPY)
 
-        def differ(t, c):
-            cols = slice(c * W, (c + 1) * W)
-            nc.scalar.activation(far[t][:, cols], dt[t][:].indirect(n3_t[:, c * 8 : (c + 1) * 8]), COPY)
-            nc.vector.tensor_tensor(dif[t][:, cols], dt[t][:, cols], far[t][:, cols], ALU.subtract)
-            nc.vector.tensor_scalar(zq[:, cols, t], dif[t][:, cols], gn_t[:, t : t + 1], None, ALU.mult)
+        def fetch_far(t, c):
+            nc.scalar.activation(far[t][:, c * W : (c + 1) * W], dt[t][:].indirect(n3_t[:, c * 8 : (c + 1) * 8]), COPY)
 
-        pick(0)
-        for t in range(4):
-            if t + 1 < 4:
-                pick(t + 1)
-            put(t)
-            if t > 0:
-                differ(t - 1, 0)
-        differ(3, 0)
+        def fetch_far_whole(t):
+            nc.scalar.activation(far[t][:], dt[t][:].indirect(n3_t[:]), COPY)
+
+        acc_a = product("h_acc0", w_early[0], sc1, 0, P)
+        nc.scalar.activation(hs[0][:], acc_a[:], COPY, scale=0.0625)
+        fetch_a(0)
+
+        raw_b1 = reuse.tile([P, H], U8, name="raw_b1", offset=0, align_bytes=64)
+        pick_half(raw_b1, d_sc[:], 1)
+        fetch_b(0)
+        deal_early(sc2[:, 0 : 2 * P], raw_b1)
+        deal_late(sc2[:, 2 * P :], raw_b1, 1)
+        settle((nc.sync, nc.sync, nc.sync), sc2)
+        raw_w1 = keep.tile([P, H], U32, name="raw_w1", tag="pa0", align_bytes=64)
+        pick_half(raw_w1, d_w[:].bitcast(U32), 1)
+        deal_early(w_early[1][:], raw_w1)
+        w_late = keep.tile([P, 4 * P], U32, name="w_late", tag="pb0", align_bytes=64)
+        deal_late(w_late[:], raw_w0, 0)
+        deal_late(w_late[:], raw_w1, 1)
+
+        gn_t = keep.tile([P, 4], F32, name="gn_t", tag="first", align_bytes=64)
+        nc.sync.dma_start(gn_t[:], gn.rearrange("(p t) o -> p (t o)", t=4))
+        w_tile = keep.tile([P, 3 * N], U8, name="w_tile", tag="raw", align_bytes=64)
+        w_w = w_tile[:, 0 : 2 * N]
+        w_sc = w_tile[:, 2 * N :]
+        nc.sync.dma_start(w_w.bitcast(I32), w1_words[0].bitcast(I32))
+
+        put_a(0)
+        put_b(0)
+        fetch_far_whole(0)
+
+        accs = [product("h_acc1", w_early[1], sc2, 0, P)]
+        for t in range(2):
+            accs.append(product("h_acc%d" % (2 + t), w_late[:, t * P :], sc2, (2 + t) * P, 2 * P))
+        for t in range(1, 4):
+            nc.vector.tensor_scalar(hs[t][:], accs[t - 1][:], 0.0625, None, ALU.mult)
+        nc.vector.memset(w_sc.bitcast(I32), 0)
+        for j in range(4):
+            nc.sync.dma_start(w_tile[j:P:32, 2 * N :].bitcast(I32), w1_scales[0][j:16:4, :].bitcast(I32))
+
+        lo, hi = slice(0, HP), slice(HP, P)
+
+        def gain(src, rows, cols, t):
+            nc.vector.tensor_scalar(zq[rows, cols, t], src[rows, cols], gn_t[rows, t : t + 1], None, ALU.mult)
+
+        every = slice(0, S)
+        dif = [keep.tile([P, S], F32, name="dif0", tag="pb0", align_bytes=64), keep.tile([P, S], F32, name="dif1")]
+        moved = keep.tile([P, S], F32, name="moved", tag="moved")
+        nc.vector.tensor_tensor(dif[0][:], dt[0][:, 0:S], far[0][:], ALU.subtract)
+        nc.sync.dma_start(moved[lo, :], dif[0][hi, :])
+        gain(dif[0], lo, every, 0)
+
+        fetch_a(1)
+        fetch_b(1)
+        fetch_a(2)
+        fetch_b(2)
+        put_a(1)
+        fetch_a(3)
+        put_b(1)
+        fetch_b(3)
+        gain(moved, lo, every, 1)
+        fetch_far_whole(1)
+        nc.vector.tensor_tensor(dif[1][:], dt[1][:, 0:S], far[1][:], ALU.subtract)
+        nc.sync.dma_start(moved[hi, :], dif[1][lo, :])
+        gain(dif[1], hi, every, 1)
+        gain(moved, hi, every, 0)
+        put_a(2)
+        put_a(3)
+        put_b(2)
+        put_b(3)
 
         zc = keep.tile([P, S], U32, name="zc", align_bytes=64)
         zs = keep.tile([P, S], U8, name="zs", align_bytes=64)
-        acc2 = [[psum.tile([P, W], F32, name="o_acc%d_%d" % (c, m), tag="o_acc%d" % m) for m in range(4)] for c in range(1)]
-        h2 = [keep.tile([P, S], F32, name="h2_%d" % m) for m in range(4)]
+        h2 = [keep.tile([P, S + SPARE], F32, name="h2_%d" % m) for m in range(4)]
+        dif_late = keep.tile([P, 2 * S], F32, name="dif_late", tag="moved")
+        neg_gn = keep.tile([P, 2], F32, name="neg_gn")
+        nc.vector.tensor_scalar(neg_gn[:], gn_t[:, 2:4], -1.0, None, ALU.mult)
+        for t in (2, 3):
+            nc.vector.tensor_scalar(dif_late[:, (t - 2) * S : (t - 1) * S], dt[t][:], gn_t[:, t : t + 1], None, ALU.mult)
 
-        def second(c):
+        def second(m, cols, name):
+            acc = psum.tile([P, cols.stop - cols.start], F32, name=name)
+            nc.tensor.matmul_mx(
+                out=acc[:],
+                lhsT=w_tile[:, 2 * P * m : 2 * P * (m + 1)].bitcast(FP4X4),
+                lhsT_scale=w_tile[:, 2 * N + P * m : 2 * N + P * (m + 1)],
+                rhs=zc[:, cols].bitcast(FP8X4),
+                rhs_scale=zs[:, cols],
+                start=True,
+                stop=True,
+            )
+            return acc
+
+        for c in range(2):
             cols = slice(c * W, (c + 1) * W)
+            for t in (2, 3):
+                fetch_far(t, c)
+                own = dif_late[:, (t - 2) * S + c * W : (t - 2) * S + (c + 1) * W]
+                nc.vector.scalar_tensor_tensor(
+                    zq[:, cols, t], far[t][:, cols], neg_gn[:, t - 2 : t - 1], own, ALU.mult, ALU.add
+                )
             nc.vector.quantize_mx(
                 out=zc[:, cols].bitcast(FP8X4), scales=zs[:, cols], in_=zq[:, cols, :].rearrange("p c t -> p (c t)")
             )
-            for m in range(4):
-                acc = acc2[0][m] if c == 0 else psum.tile([P, W], F32, name="o_accb%d" % m, tag="h_acc%d" % m)
-                nc.tensor.matmul_mx(
-                    out=acc[:],
-                    lhsT=w_w[:, 2 * P * m : 2 * P * (m + 1)].bitcast(FP4X4),
-                    lhsT_scale=w_sc[:, P * m : P * (m + 1)],
-                    rhs=zc[:, cols].bitcast(FP8X4),
-                    rhs_scale=zs[:, cols],
-                    start=True,
-                    stop=True,
-                )
-                nc.vector.tensor_copy(h2[m][:, cols], acc[:])
-
-        second(0)
-        for t in range(4):
-            differ(t, 1)
-        second(1)
+            nc.scalar.copy(h2[0][:, cols], second(0, cols, "o_half%d" % c)[:])
+        for m in range(1, 4):
+            nc.vector.tensor_copy(h2[m][:, 0:S], second(m, every, "h_acc%d" % m)[:])
 
         near = [keep.tile([P, S], F32, name="near%d" % m) for m in range(4)]
         nw = [keep.tile([P, S], F32, name="nw%d" % m) for m in range(4)]
 
         def look(m):
-            for c in range(2):
-                nc.scalar.activation(near[m][:, c * W : (c + 1) * W], h2[m][:].indirect(n5_t[:, c * 8 : (c + 1) * 8]), COPY)
-            nc.vector.tensor_tensor(nw[m][:], h2[m][:], near[m][:], ALU.max)
+            nc.scalar.activation(near[m][:], h2[m][:].indirect(n5_t[:]), COPY)
+            nc.vector.tensor_tensor(nw[m][:], h2[m][:, 0:S], near[m][:], ALU.max)
 
         def leave(m):
             nc.scalar.activation(pages[m][:].indirect(n4_t[:]), nw[m][:], COPY)

@@ -38,7 +38,7 @@ def tile_picked_aqlorddpags_none_p_kernel(
         def load_scales(src, name):
             rows = src[0].bitcast(I32)
             tl = keep.tile([P, src.shape[2]], U8, name=name, align_bytes=64)
-            nc.sync.dma_start(tl[:].bitcast(I32), rows.unsqueeze(1).to_broadcast([16, 8, rows.shape[1]]))
+            nc.scalar.dma_start(tl[:].bitcast(I32), rows.unsqueeze(1).to_broadcast([16, 8, rows.shape[1]]))
             return tl
 
         def load_words(src, tl):
@@ -71,13 +71,13 @@ def tile_picked_aqlorddpags_none_p_kernel(
                 pick(raw[:, l * HALF : (l + 1) * HALF], window, l, hf)
 
         def entries(raw, t0):
-            return raw[:, 0:H].rearrange("p (l m t) -> p l m t", l=2, t=4)[:, :, :, t0 : t0 + 2]
+            return raw.rearrange("p (l m t) -> p l m t", m=HP, t=4)[:, :, :, t0 : t0 + 2]
 
         def deal_early(dst, raw):
-            nc.vector.tensor_copy(dst.rearrange("p (l t m) -> p l m t", l=2, t=2), entries(raw, 0))
+            nc.vector.tensor_copy(dst.rearrange("p (l t m) -> p l m t", m=HP, t=2), entries(raw, 0))
 
         def deal_late(dst, raw, hf):
-            view = dst.rearrange("p (l t m) -> p l m t", l=2, t=2)[:, :, hf * HP : (hf + 1) * HP, :]
+            view = dst.rearrange("p (l t m) -> p l m t", m=P, t=2)[:, :, hf * HP : (hf + 1) * HP, :]
             nc.vector.tensor_copy(view, entries(raw, 2))
 
         def settle(queues, plane):
@@ -85,7 +85,7 @@ def tile_picked_aqlorddpags_none_p_kernel(
                 queue.dma_start(plane[j:P:32, :].bitcast(I32), plane[8 * j : P : 32, :].bitcast(I32))
 
         sc1 = keep.tile([P, 2 * P + S], U8, name="sc1", align_bytes=64)
-        sc2 = reuse.tile([P, 6 * P], U8, name="sc2", offset=1024, align_bytes=64)
+        sc2 = keep.tile([P, 6 * P], U8, name="sc2", align_bytes=64)
         w_early = [keep.tile([P, 2 * P], U32, name="w_early%d" % hf, align_bytes=64) for hf in range(2)]
         xw = keep.tile([P, S], U32, name="xw", align_bytes=64)
 
@@ -93,14 +93,14 @@ def tile_picked_aqlorddpags_none_p_kernel(
         nc.vector.tensor_copy(raw_b0[:, H : H + S], x_sc[:].indirect(offs_t[:]))
         pick_half(raw_b0, d_sc[:], 0)
         nc.vector.tensor_copy(sc1[:, 2 * P :].bitcast(I32), raw_b0[:, H : H + S].bitcast(I32))
-        deal_early(sc1[:, 0 : 2 * P], raw_b0)
+        deal_early(sc1[:, 0 : 2 * P], raw_b0[:, 0:H])
         settle((nc.sync, nc.scalar, nc.sync), sc1)
+        deal_late(sc2[:, 2 * P :], raw_b0[:, 0:H], 0)
 
         raw_w0 = keep.tile([P, H], U32, name="raw_w0", tag="raw", align_bytes=64)
         pick_half(raw_w0, d_w[:].bitcast(U32), 0)
-        deal_early(w_early[0][:], raw_w0)
+        deal_early(w_early[0][:], raw_w0[:])
         nc.vector.tensor_copy(xw[:], x_w[:].bitcast(U32).indirect(offs_t[:]))
-        deal_late(sc2[:, 2 * P :], raw_b0, 0)
 
         def product(name, words, plane, c0, step):
             acc = psum.tile([P, S], F32, name=name)
@@ -116,7 +116,7 @@ def tile_picked_aqlorddpags_none_p_kernel(
                 )
             return acc
 
-        hs = [keep.tile([P, S], F32, name="h%d" % t) for t in range(4)]
+        hs = [keep.tile([P, S], F32, name="h%d" % t) for t in range(3)]
         zq = keep.tile([P, S, 4], BF16, name="zq", align_bytes=64)
         pa = [keep.tile([P, W], F32, name="pa%d" % t, tag="pa%d" % t, align_bytes=64) for t in range(4)]
         pb = [keep.tile([P, W], F32, name="pb%d" % t, tag="pb%d" % t, align_bytes=64) for t in range(4)]
@@ -154,15 +154,21 @@ def tile_picked_aqlorddpags_none_p_kernel(
         raw_b1 = reuse.tile([P, H], U8, name="raw_b1", offset=0, align_bytes=64)
         pick_half(raw_b1, d_sc[:], 1)
         fetch_b(0)
-        deal_early(sc2[:, 0 : 2 * P], raw_b1)
-        deal_late(sc2[:, 2 * P :], raw_b1, 1)
+        deal_early(sc2[:, 0 : 2 * P], raw_b1[:])
+        deal_late(sc2[:, 2 * P :], raw_b1[:], 1)
         settle((nc.sync, nc.sync, nc.sync), sc2)
-        raw_w1 = keep.tile([P, H], U32, name="raw_w1", tag="pa0", align_bytes=64)
-        pick_half(raw_w1, d_w[:].bitcast(U32), 1)
-        deal_early(w_early[1][:], raw_w1)
+        raw_w1 = [
+            reuse.tile([P, HALF], U32, name="raw_w1a", offset=0, align_bytes=64),
+            keep.tile([P, HALF], U32, name="raw_w1b", tag="pa0", align_bytes=64),
+        ]
+        for l in range(2):
+            pick(raw_w1[l][:], d_w[:].bitcast(U32), l, 1)
+        for l in range(2):
+            deal_early(w_early[1][:, l * P : (l + 1) * P], raw_w1[l][:])
         w_late = keep.tile([P, 4 * P], U32, name="w_late", tag="pb0", align_bytes=64)
-        deal_late(w_late[:], raw_w0, 0)
-        deal_late(w_late[:], raw_w1, 1)
+        deal_late(w_late[:], raw_w0[:], 0)
+        for l in range(2):
+            deal_late(w_late[:, 2 * l * P : 2 * (l + 1) * P], raw_w1[l][:], 1)
 
         gn_t = keep.tile([P, 4], F32, name="gn_t", tag="first", align_bytes=64)
         nc.sync.dma_start(gn_t[:], gn.rearrange("(p t) o -> p (t o)", t=4))
@@ -178,7 +184,7 @@ def tile_picked_aqlorddpags_none_p_kernel(
         accs = [product("h_acc1", w_early[1], sc2, 0, P)]
         for t in range(2):
             accs.append(product("h_acc%d" % (2 + t), w_late[:, t * P :], sc2, (2 + t) * P, 2 * P))
-        for t in range(1, 4):
+        for t in range(1, 3):
             nc.vector.tensor_scalar(hs[t][:], accs[t - 1][:], 0.0625, None, ALU.mult)
         nc.vector.memset(w_sc.bitcast(I32), 0)
         for j in range(4):
@@ -198,6 +204,8 @@ def tile_picked_aqlorddpags_none_p_kernel(
 
         fetch_a(1)
         fetch_b(1)
+        hs.append(keep.tile([P, S], F32, name="h3", tag="pa1", align_bytes=64))
+        nc.vector.tensor_scalar(hs[3][:], accs[2][:], 0.0625, None, ALU.mult)
         fetch_a(2)
         fetch_b(2)
         put_a(1)

@@ -57,11 +57,9 @@ def tile_picked_aqlorddpags_none_p_kernel(
         n5_t = load_list(n5, "n5_t")
         n4_t = load_list(n4, "n4_t")
 
-        pages = [keep.tile([P, U], F32, name="page%d" % i) for i in range(4)]
-        nc.gpsimd.memset(pages[0][:].bitcast(I32), 0)
-        nc.gpsimd.memset(pages[1][:].bitcast(I32), 0)
-        nc.vector.memset(pages[2][:].bitcast(I32), 0)
-        nc.vector.memset(pages[3][:].bitcast(I32), 0)
+        pages = [keep.tile([P, U], F32, name="page%d" % i) for i in range(2)]
+        for page in pages:
+            nc.vector.memset(page[:].bitcast(I32), 0)
 
         def pick(dst, window, l, hf):
             nc.vector.tensor_copy(dst, window.indirect(codes[l][:, hf * 16 : (hf + 1) * 16]))
@@ -225,7 +223,7 @@ def tile_picked_aqlorddpags_none_p_kernel(
 
         zc = keep.tile([P, S], U32, name="zc", align_bytes=64)
         zs = keep.tile([P, S], U8, name="zs", align_bytes=64)
-        h2 = [keep.tile([P, S + SPARE], F32, name="h2_%d" % m) for m in range(4)]
+        h2 = [keep.tile([P, S + SPARE], F32, name="h2_%d" % m, tag="h2_%d" % m) for m in range(4)]
         dif_late = keep.tile([P, 2 * S], F32, name="dif_late", tag="moved")
         neg_gn = keep.tile([P, 2], F32, name="neg_gn")
         nc.vector.tensor_scalar(neg_gn[:], gn_t[:, 2:4], -1.0, None, ALU.mult)
@@ -275,4 +273,7 @@ def tile_picked_aqlorddpags_none_p_kernel(
         for m in range(4):
             if m + 1 < 4:
                 look(m + 1)
+            if m < 2:
+                pages.append(keep.tile([P, U], F32, name="page%d" % (m + 2), tag="h2_%d" % m))
+                nc.vector.memset(pages[m + 2][:].bitcast(I32), 0)
             leave(m)

from contextlib import ExitStack

import concourse.mybir as mybir

K, T, S, N, G, H, W, U = 512, 1024, 256, 512, 2048, 512, 128, 1024
FLOPS = 2 * 2 * K * H * S + 2 * H * N * S

F32 = mybir.dt.float32
BF16 = mybir.dt.bfloat16
I32 = mybir.dt.int32
U32 = mybir.dt.uint32
U16 = mybir.dt.uint16
U8 = mybir.dt.uint8
FP8X4 = mybir.dt.float8_e4m3fn_x4
FP4X4 = mybir.dt.float4_e2m1fn_x4
ALU = mybir.AluOpType
COPY = mybir.ActivationFunctionType.Copy
P = 128
HP = 64
HALF = H // 2
SPARE = 16


def tile_picked_aqlorddpags_none_p_kernel(
    tc, x_words, x_scales, d_words, d_scales, gn, w1_words, w1_scales, offs, ka, kb, n1, n2, n3, n4, n5, out
):
    nc = tc.nc
    with ExitStack() as ctx:
        keep = ctx.enter_context(tc.tile_pool(name="keep", bufs=1))
        reuse = ctx.enter_context(tc.tile_pool(name="reuse", bufs=1))
        psum = ctx.enter_context(tc.psum_pool(name="psum", bufs=1))

        def load_list(src, name):
            tl = keep.tile([P, src.shape[1]], U16, name=name)
            nc.sync.dma_start(tl[:], src)
            return tl

        def load_scales(src, name):
            rows = src[0].bitcast(I32)
            tl = keep.tile([P, src.shape[2]], U8, name=name, align_bytes=64)
            nc.scalar.dma_start(tl[:].bitcast(I32), rows.unsqueeze(1).to_broadcast([16, 8, rows.shape[1]]))
            return tl

        def load_words(src, tl):
            nc.sync.dma_start(tl[:], src[0].rearrange("p n t -> p (n t)").bitcast(I32))
            return tl

        offs_t = load_list(offs, "offs_t")
        x_sc = load_scales(x_scales, "x_sc")
        codes = [load_list(ka, "ka_t"), load_list(kb, "kb_t")]
        d_sc = load_scales(d_scales, "d_sc")
        n1_t = load_list(n1, "n1_t")
        n2_t = load_list(n2, "n2_t")
        d_w = load_words(d_words, keep.tile([P, G], I32, name="d_w", align_bytes=64))
        x_w = load_words(x_words, reuse.tile([P, T], I32, name="x_w", offset=0, align_bytes=64))
        n3_t = load_list(n3, "n3_t")
        n5_t = load_list(n5, "n5_t")
        n4_t = load_list(n4, "n4_t")

        pages = [keep.tile([P, U], F32, name="page%d" % i) for i in range(2)]
        for page in pages:
            nc.vector.memset(page[:].bitcast(I32), 0)

        def pick(dst, window, l, hf):
            nc.vector.tensor_copy(dst, window.indirect(codes[l][:, hf * 16 : (hf + 1) * 16]))

        def pick_half(raw, window, hf):
            for l in range(2):
                pick(raw[:, l * HALF : (l + 1) * HALF], window, l, hf)

        def entries(raw, t0):
            return raw.rearrange("p (l m t) -> p l m t", m=HP, t=4)[:, :, :, t0 : t0 + 2]

        def deal_early(dst, raw):
            nc.vector.tensor_copy(dst.rearrange("p (l t m) -> p l m t", m=HP, t=2), entries(raw, 0))

        def deal_late(dst, raw, hf):
            view = dst.rearrange("p (l t m) -> p l m t", m=P, t=2)[:, :, hf * HP : (hf + 1) * HP, :]
            nc.vector.tensor_copy(view, entries(raw, 2))

        def settle(queues, plane):
            for j, queue in zip(range(1, 4), queues):
                queue.dma_start(plane[j:P:32, :].bitcast(I32), plane[8 * j : P : 32, :].bitcast(I32))

        sc1 = keep.tile([P, 2 * P + S], U8, name="sc1", align_bytes=64)
        sc2 = keep.tile([P, 6 * P], U8, name="sc2", align_bytes=64)
        w_early = [keep.tile([P, 2 * P], U32, name="w_early%d" % hf, align_bytes=64) for hf in range(2)]
        xw = keep.tile([P, S], U32, name="xw", align_bytes=64)

        raw_b0 = keep.tile([P, H + S], U8, name="raw_b0", tag="first", align_bytes=64)
        nc.vector.tensor_copy(raw_b0[:, H : H + S], x_sc[:].indirect(offs_t[:]))
        pick_half(raw_b0, d_sc[:], 0)
        nc.vector.tensor_copy(sc1[:, 2 * P :].bitcast(I32), raw_b0[:, H : H + S].bitcast(I32))
        deal_early(sc1[:, 0 : 2 * P], raw_b0[:, 0:H])
        settle((nc.sync, nc.scalar, nc.sync), sc1)
        deal_late(sc2[:, 2 * P :], raw_b0[:, 0:H], 0)

        raw_w0 = keep.tile([P, H], U32, name="raw_w0", tag="raw", align_bytes=64)
        pick_half(raw_w0, d_w[:].bitcast(U32), 0)
        deal_early(w_early[0][:], raw_w0[:])
        nc.vector.tensor_copy(xw[:], x_w[:].bitcast(U32).indirect(offs_t[:]))

        def product(name, words, plane, c0, step):
            acc = psum.tile([P, S], F32, name=name)
            for l in range(2):
                nc.tensor.matmul_mx(
                    out=acc[:],
                    lhsT=words[:, l * step : l * step + P].bitcast(FP8X4),
                    lhsT_scale=plane[:, c0 + l * step : c0 + l * step + P],
                    rhs=xw[:].bitcast(FP8X4),
                    rhs_scale=sc1[:, 2 * P :],
                    start=(l == 0),
                    stop=(l == 1),
                )
            return acc

        hs = [keep.tile([P, S], F32, name="h%d" % t) for t in range(3)]
        zq = keep.tile([P, S, 4], BF16, name="zq", align_bytes=64)
        pa = [keep.tile([P, W], F32, name="pa%d" % t, tag="pa%d" % t, align_bytes=64) for t in range(4)]
        pb = [keep.tile([P, W], F32, name="pb%d" % t, tag="pb%d" % t, align_bytes=64) for t in range(4)]
        ra = [keep.tile([P, W], F32, name="ra%d" % t) for t in range(2)]
        ra.extend(reuse.tile([P, W], F32, name="ra%d" % t, offset=4096 + 512 * (t - 2)) for t in (2, 3))
        rb = {t: keep.tile([P, W], F32, name="rb%d" % t) for t in (0, 2, 3)}
        rb[1] = reuse.tile([P, W], F32, name="rb_held", offset=4096 + 256)
        dt = [keep.tile([P, S + SPARE * (t < 2)], F32, name="dt%d" % t) for t in range(4)]
        far = [keep.tile([P, S], F32, name="far%d" % t) for t in range(4)]

        def fetch_a(t):
            nc.scalar.activation(pa[t][:], hs[t][:].indirect(n1_t[:]), COPY)

        def fetch_b(t):
            nc.scalar.activation(pb[t][:], hs[t][:].indirect(n2_t[:]), COPY)
            nc.vector.tensor_tensor(ra[t][:], pa[t][:], pb[t][:], ALU.max)
            nc.vector.tensor_tensor(rb[t][:], pa[t][:], pb[t][:], ALU.min)

        def put_a(t):
            nc.scalar.activation(dt[t][:].indirect(n1_t[:]), ra[t][:], COPY)

        def put_b(t):
            nc.scalar.activation(dt[t][:].indirect(n2_t[:]), rb[t][:], COPY)

        def fetch_far(t, c):
            nc.scalar.activation(far[t][:, c * W : (c + 1) * W], dt[t][:].indirect(n3_t[:, c * 8 : (c + 1) * 8]), COPY)

        def fetch_far_whole(t):
            nc.scalar.activation(far[t][:], dt[t][:].indirect(n3_t[:]), COPY)

        acc_a = product("h_acc0", w_early[0], sc1, 0, P)
        nc.scalar.activation(hs[0][:], acc_a[:], COPY, scale=0.0625)
        fetch_a(0)

        raw_b1 = reuse.tile([P, H], U8, name="raw_b1", offset=0, align_bytes=64)
        pick_half(raw_b1, d_sc[:], 1)
        fetch_b(0)
        deal_early(sc2[:, 0 : 2 * P], raw_b1[:])
        deal_late(sc2[:, 2 * P :], raw_b1[:], 1)
        settle((nc.sync, nc.sync, nc.sync), sc2)
        raw_w1 = [
            reuse.tile([P, HALF], U32, name="raw_w1a", offset=0, align_bytes=64),
            keep.tile([P, HALF], U32, name="raw_w1b", tag="pa0", align_bytes=64),
        ]
        for l in range(2):
            pick(raw_w1[l][:], d_w[:].bitcast(U32), l, 1)
        for l in range(2):
            deal_early(w_early[1][:, l * P : (l + 1) * P], raw_w1[l][:])
        w_late = keep.tile([P, 4 * P], U32, name="w_late", tag="pb0", align_bytes=64)
        deal_late(w_late[:], raw_w0[:], 0)
        for l in range(2):
            deal_late(w_late[:, 2 * l * P : 2 * (l + 1) * P], raw_w1[l][:], 1)

        gn_t = keep.tile([P, 4], F32, name="gn_t", tag="first", align_bytes=64)
        nc.sync.dma_start(gn_t[:], gn.rearrange("(p t) o -> p (t o)", t=4))
        w_tile = keep.tile([P, 3 * N], U8, name="w_tile", tag="raw", align_bytes=64)
        w_w = w_tile[:, 0 : 2 * N]
        w_sc = w_tile[:, 2 * N :]
        nc.sync.dma_start(w_w.bitcast(I32), w1_words[0].bitcast(I32))

        put_a(0)
        put_b(0)
        fetch_far_whole(0)

        accs = [product("h_acc1", w_early[1], sc2, 0, P)]
        for t in range(2):
            accs.append(product("h_acc%d" % (2 + t), w_late[:, t * P :], sc2, (2 + t) * P, 2 * P))
        for t in range(1, 3):
            nc.vector.tensor_scalar(hs[t][:], accs[t - 1][:], 0.0625, None, ALU.mult)
        nc.vector.memset(w_sc.bitcast(I32), 0)
        for j in range(4):
            nc.sync.dma_start(w_tile[j:P:32, 2 * N :].bitcast(I32), w1_scales[0][j:16:4, :].bitcast(I32))

        lo, hi = slice(0, HP), slice(HP, P)

        def gain(src, rows, cols, t):
            nc.vector.tensor_scalar(zq[rows, cols, t], src[rows, cols], gn_t[rows, t : t + 1], None, ALU.mult)

        every = slice(0, S)
        dif = [keep.tile([P, S], F32, name="dif0", tag="pb0", align_bytes=64), keep.tile([P, S], F32, name="dif1")]
        moved = keep.tile([P, S], F32, name="moved", tag="moved")
        nc.vector.tensor_tensor(dif[0][:], dt[0][:, 0:S], far[0][:], ALU.subtract)
        nc.sync.dma_start(moved[lo, :], dif[0][hi, :])
        gain(dif[0], lo, every, 0)

        fetch_a(1)
        fetch_b(1)
        hs.append(keep.tile([P, S], F32, name="h3", tag="pa1", align_bytes=64))
        nc.vector.tensor_scalar(hs[3][:], accs[2][:], 0.0625, None, ALU.mult)
        fetch_a(2)
        fetch_b(2)
        put_a(1)
        fetch_a(3)
        put_b(1)
        fetch_b(3)
        gain(moved, lo, every, 1)
        fetch_far_whole(1)
        nc.vector.tensor_tensor(dif[1][:], dt[1][:, 0:S], far[1][:], ALU.subtract)
        nc.sync.dma_start(moved[hi, :], dif[1][lo, :])
        gain(dif[1], hi, every, 1)
        gain(moved, hi, every, 0)
        put_a(2)
        put_a(3)
        put_b(2)
        put_b(3)

        zc = keep.tile([P, S], U32, name="zc", align_bytes=64)
        zs = keep.tile([P, S], U8, name="zs", align_bytes=64)
        h2 = [keep.tile([P, S + SPARE], F32, name="h2_%d" % m, tag="h2_%d" % m) for m in range(4)]
        dif_late = keep.tile([P, 2 * S], F32, name="dif_late", tag="moved")
        neg_gn = keep.tile([P, 2], F32, name="neg_gn")
        nc.vector.tensor_scalar(neg_gn[:], gn_t[:, 2:4], -1.0, None, ALU.mult)
        for t in (2, 3):
            nc.vector.tensor_scalar(dif_late[:, (t - 2) * S : (t - 1) * S], dt[t][:], gn_t[:, t : t + 1], None, ALU.mult)

        def second(m, cols, name):
            acc = psum.tile([P, cols.stop - cols.start], F32, name=name)
            nc.tensor.matmul_mx(
                out=acc[:],
                lhsT=w_tile[:, 2 * P * m : 2 * P * (m + 1)].bitcast(FP4X4),
                lhsT_scale=w_tile[:, 2 * N + P * m : 2 * N + P * (m + 1)],
                rhs=zc[:, cols].bitcast(FP8X4),
                rhs_scale=zs[:, cols],
                start=True,
                stop=True,
            )
            return acc

        for c in range(2):
            cols = slice(c * W, (c + 1) * W)
            for t in (2, 3):
                fetch_far(t, c)
                own = dif_late[:, (t - 2) * S + c * W : (t - 2) * S + (c + 1) * W]
                nc.vector.scalar_tensor_tensor(
                    zq[:, cols, t], far[t][:, cols], neg_gn[:, t - 2 : t - 1], own, ALU.mult, ALU.add
                )
            nc.vector.quantize_mx(
                out=zc[:, cols].bitcast(FP8X4), scales=zs[:, cols], in_=zq[:, cols, :].rearrange("p c t -> p (c t)")
            )
            nc.scalar.copy(h2[0][:, cols], second(0, cols, "o_half%d" % c)[:])
        for m in range(1, 4):
            nc.vector.tensor_copy(h2[m][:, 0:S], second(m, every, "h_acc%d" % m)[:])

        near = [keep.tile([P, S], F32, name="near%d" % m) for m in range(4)]
        nw = [keep.tile([P, S], F32, name="nw%d" % m) for m in range(4)]

        def look(m):
            nc.scalar.activation(near[m][:], h2[m][:].indirect(n5_t[:]), COPY)
            nc.vector.tensor_tensor(nw[m][:], h2[m][:, 0:S], near[m][:], ALU.max)

        def leave(m):
            nc.scalar.activation(pages[m][:].indirect(n4_t[:]), nw[m][:], COPY)
            nc.sync.dma_start(out[m * P : (m + 1) * P, :], pages[m][:])

        look(0)
        for m in range(4):
            if m + 1 < 4:
                look(m + 1)
            if m < 2:
                pages.append(keep.tile([P, U], F32, name="page%d" % (m + 2), tag="h2_%d" % m))
                nc.vector.memset(pages[m + 2][:].bitcast(I32), 0)
            leave(m)
